import numpy as np
import ml_dtypes


def mxq(x, axis, fmt="e4m3"):
    dtype, down = {"e4m3": (ml_dtypes.float8_e4m3fn, 7), "e5m2": (ml_dtypes.float8_e5m2, 14)}[fmt]
    v = np.moveaxis(np.asarray(x, np.float32).astype(ml_dtypes.bfloat16).astype(np.float64), axis, -1)
    blocks = v.reshape(v.shape[:-1] + (-1, 32))
    amax = np.abs(blocks).max(-1, keepdims=True)
    byte = np.maximum(np.where(amax > 0, np.frexp(amax)[1] - 1 + 127, 0) - down, 1)
    scale = np.exp2(byte - 127.0)
    codes = (blocks / scale).astype(np.float32).astype(dtype).astype(np.float64)
    return np.moveaxis((codes * scale).reshape(v.shape), -1, axis)


WIDE = False


def mx_kscale(k):
    if not WIDE:
        return np.ones(k)
    levels = np.array([10, -10, 5, -5, 0])
    if k % 512:
        return np.exp2(np.random.permutation(np.resize(levels, k // 32))).repeat(32)
    a = np.empty((k // 512, 16))
    for p in range(k // 512):
        a[p, :8] = np.random.permutation(np.resize(levels, 8))
        for g in range(8):
            far = levels[np.abs(levels - a[p, g]) >= 10]
            a[p, g + 8] = far[np.random.randint(len(far))]
    return np.exp2(a.ravel()).repeat(32)


def f64(x):
    return np.asarray(x).astype(np.float64)


def striped(idx):
    return np.tile(np.asarray(idx).reshape(-1, 16).T, (8, 1)).astype(np.uint16)


def unstriped(offs):
    return offs[:16].T.reshape(-1).astype(np.int64)


E2M1 = np.array([0.0, 0.5, 1.0, 1.5, 2.0, 3.0, 4.0, 6.0, -0.0, -0.5, -1.0, -1.5, -2.0, -3.0, -4.0, -6.0])


def pack_weight(w, fmt):
    k, n = w.shape
    w = f64(np.asarray(w, np.float32).astype(ml_dtypes.bfloat16)).reshape(k // 32, 32, n)
    amax = np.abs(w).max(1)
    if fmt == "e4m3":
        byte = np.frexp(amax)[1] - 1 + 127 - 7
    else:
        mant, ex = np.frexp(amax / 6.0)
        byte = np.where(mant > 0.5, ex, ex - 1) + 127
    byte = np.clip(np.where(amax > 0, byte, 1), 1, 254)
    scaled = (w * np.exp2(127.0 - byte)[:, None, :]).reshape(k, n).astype(np.float32)
    by_word = np.ascontiguousarray(scaled.reshape(k // 512, 128, 4, n).transpose(0, 1, 3, 2))
    if fmt == "e4m3":
        words = by_word.astype(ml_dtypes.float8_e4m3fn).view(np.uint8)
    else:
        c = by_word.astype(ml_dtypes.float4_e2m1fn).view(np.uint8) & 0xF
        words = (c[..., 0::2] | (c[..., 1::2] << 4)).reshape(k // 512, 128, 2 * n)
    return np.ascontiguousarray(words), np.ascontiguousarray(byte.astype(np.uint8).reshape(k // 512, 16, n))


def unpack_weight(words, scales, fmt):
    g, _, n = scales.shape
    words = np.ascontiguousarray(words).reshape(g, 128, n, -1)
    if fmt == "e4m3":
        vals = words.view(ml_dtypes.float8_e4m3fn).astype(np.float64)
    else:
        nib = np.empty((g, 128, n, 4), np.uint8)
        nib[..., 0::2] = words & 0xF
        nib[..., 1::2] = words >> 4
        vals = E2M1[nib]
    vals = vals * np.repeat(np.exp2(scales.astype(np.float64) - 127.0), 8, axis=1)[..., None]
    return vals.transpose(0, 1, 3, 2).reshape(g * 512, n)


def sigmoid(v):
    return 1.0 / (1.0 + np.exp(-v))


D, T, I, Q, E, M = 512, 2048, 512, 512, 512, 1024


def setup_inputs():
    n = np.random.standard_normal
    idx = np.random.permutation(T)[:I]
    idx2 = np.random.permutation(M)[:I]
    fd = mx_kscale(D)
    fq = mx_kscale(Q)
    keysp = pack_weight(n((D, T)) / fd[:, None], "e2m1")
    return {
        "query": (n((D, Q)) * 1.0 / np.sqrt(D) * fd[:, None]).astype(np.float32),
        "query2": (n((D, Q)) * 1.0 / np.sqrt(D) * fd[:, None]).astype(np.float32),
        "query3": (n((D, Q)) * 0.8 / np.sqrt(D) * fd[:, None]).astype(np.float32),
        "keys_words": keysp[0],
        "keys_scales": keysp[1],
        "eager": (np.random.uniform(0.8, 2.0, (Q, 1))).astype(np.float32),
        "thresh": (np.random.uniform(1.5, 4.0, (Q, 1))).astype(np.float32),
        "qs": (np.random.uniform(20.0, 80.0, (Q, 1)) * fq[:, None]).astype(np.float32),
        "msgs": (n((Q, E)) * 1 / np.sqrt(Q) / fq[:, None]).astype(np.float32),
        "old": (n((E, M)) * 1.0).astype(np.float32),
        "fade": (np.random.uniform(0.3, 0.9, (1, M))).astype(np.float32),
        "offs": striped(idx),
        "offs2": striped(idx2),
    }


def reference(query, query2, query3, keys_words, keys_scales, eager, thresh, qs, msgs, old, fade, offs, offs2):
    idx = unstriped(offs)
    idx2 = unstriped(offs2)
    keysu = unpack_weight(keys_words, keys_scales, "e2m1")
    queryq = mxq(f64(query), 0, "e4m3")
    keysidxg = keysu[:, idx]
    a = queryq.T @ keysidxg
    query2q = mxq(f64(query2), 0, "e4m3")
    b = query2q.T @ keysidxg
    query3q = mxq(f64(query3), 0, "e4m3")
    b3 = query3q.T @ keysidxg
    s = a * sigmoid(b - b3) + b3
    m0 = np.max(s, axis=1, keepdims=True)
    m1 = np.mean(s, axis=1, keepdims=True)
    p = np.exp(s - m0)
    gt0 = sigmoid((m0 - m1) * f64(eager) - f64(thresh))
    w = p / np.sum(p, axis=1, keepdims=True) * gt0
    wq = w * f64(qs)
    msgsq = mxq(f64(msgs), 0, "e4m3")
    wqq = mxq(wq, 0, "e4m3")
    dl = msgsq.T @ wqq
    df = np.zeros((E, M))
    df[:, idx2] = dl
    y = f64(old) * f64(fade) + df
    return y

@@ -1,0 +1,319 @@
+from contextlib import ExitStack
+
+import concourse.mybir as mybir
+from concourse.masks import make_identity
+
+D, T, I, Q, E, M = 512, 2048, 512, 512, 512, 1024
+FLOPS = 2 * (3 * D * Q * I + Q * E * I)
+
+F32 = mybir.dt.float32
+BF16 = mybir.dt.bfloat16
+I32 = mybir.dt.int32
+U32 = mybir.dt.uint32
+U16 = mybir.dt.uint16
+U8 = mybir.dt.uint8
+FP8X4 = mybir.dt.float8_e4m3fn_x4
+FP4X4 = mybir.dt.float4_e2m1fn_x4
+ALU = mybir.AluOpType
+ACT = mybir.ActivationFunctionType
+AX = mybir.AxisListType
+
+P = 128
+PACK = 4
+RUNS = 32
+BANK = 512
+ROW_EAGER, ROW_THRESH, ROW_QS, ROW_FADE = 0, 4, 8, 16
+
+
+def tile_attend_threeviews_abstaining_delivered_kernel(
+    tc, query, query2, query3, keys_words, keys_scales, eager, thresh, qs, msgs, old, fade, offs, offs2, out
+):
+    nc = tc.nc
+    with ExitStack() as ctx:
+        keep = ctx.enter_context(tc.tile_pool(name="keep", bufs=1))
+        ring = ctx.enter_context(tc.tile_pool(name="ring", bufs=2))
+        psum = ctx.enter_context(tc.psum_pool(name="psum", bufs=4))
+
+        def sb(shape, dtype, name):
+            return keep.tile(shape, dtype, name=name, align_bytes=64)
+
+        def bank(pair):
+            return psum.tile([P, BANK], F32, name=pair)
+
+        key_bytes = sb([P, T], U8, "key_bytes")
+        nc.gpsimd.memset(key_bytes[:].bitcast(I32), 0)
+        rows = sb([P, P], F32, "rows")
+        nc.vector.memset(rows[:], 0.0)
+        windows = [sb([P, M], F32, "window%d" % w) for w in range(E // P)]
+        for w in windows[:2]:
+            nc.vector.memset(w[:], 0.0)
+        ident = sb([P, P], F32, "ident")
+        make_identity(nc, ident[:])
+        for w in windows[2:]:
+            nc.gpsimd.memset(w[:], 0.0)
+
+        half = Q // 2
+        key_list = keep.tile([P, I // 16], U16, name="key_list")
+        nc.sync.dma_start(key_list[:], offs)
+        key_words = sb([P, T], U16, "key_words")
+        nc.sync.dma_start(out=key_words[:].bitcast(I32), in_=keys_words[0].bitcast(I32))
+        for quad in range(4):
+            nc.sync.dma_start(
+                out=key_bytes[32 * quad : 32 * quad + 4, :].bitcast(I32),
+                in_=keys_scales[0, 4 * quad : 4 * quad + 4, :].bitcast(I32),
+            )
+        fade_cols = sb([P, M // P], F32, "fade_cols")
+        nc.sync.dma_start(out=fade_cols[:], in_=fade.rearrange("o (p j) -> (o p) j", p=P))
+        raw3, raw2, raw1 = [], [], []
+        for src, dst, name in ((query3, raw3, "raw3"), (query2, raw2, "raw2"), (query, raw1, "raw1")):
+            for h in range(2):
+                t = sb([P, PACK, half], F32, "%s_%d" % (name, h))
+                nc.sync.dma_start(
+                    out=t[:], in_=src.rearrange("(p j) q -> p j q", j=PACK)[:, :, h * half : (h + 1) * half]
+                )
+                dst.append(t)
+        for vec, row in ((eager, ROW_EAGER), (thresh, ROW_THRESH), (qs, ROW_QS)):
+            nc.sync.dma_start(
+                out=rows[row : row + PACK, :].rearrange("r (c u) -> r c u", u=PACK),
+                in_=vec.rearrange("(c r u) o -> r c (u o)", r=PACK, u=PACK),
+            )
+        raw_m = sb([P, PACK, E], F32, "raw_m")
+        for u in range(PACK):
+            nc.sync.dma_start(
+                out=raw_m[u:P:PACK, :, :],
+                in_=msgs.rearrange("(c r u) e -> u c r e", r=PACK, u=PACK)[u],
+            )
+        olds = []
+        for k in range(E // P):
+            t = sb([P, M], F32, "old%d" % k)
+            nc.sync.dma_start(out=t[:], in_=old[k * P : (k + 1) * P, :])
+            olds.append(t)
+        slot_list = keep.tile([P, I // 16], U16, name="slot_list")
+        nc.sync.dma_start(slot_list[:], offs2)
+
+        warm = sb([P, 1], F32, "warm")
+        nc.scalar.activation(out=warm[:], in_=rows[:, P - 1 : P], func=ACT.Tanh)
+
+        fade_rows = sb([P, P, M // P], F32, "fade_rows")
+        for b in range(2):
+            fb = bank("ring_b")
+            for jj in range(4):
+                j = 4 * b + jj
+                nc.tensor.transpose(fb[:, jj * P : (jj + 1) * P], fade_cols[:, j : j + 1].to_broadcast([P, P]), ident[:])
+            nc.scalar.copy(out=fade_rows[:, :, 4 * b : 4 * b + 4], in_=fb[:].rearrange("x (j p) -> x p j", p=P))
+
+        kw = sb([P, I], U16, "kw")
+        nc.vector.tensor_copy(kw[:], key_words[:].indirect(key_list[:]))
+        kb = sb([P, I], U8, "kb")
+        nc.vector.tensor_copy(kb[:], key_bytes[:].indirect(key_list[:]))
+
+        def woven(name):
+            return sb([P, PACK, RUNS, PACK, PACK], BF16, name)
+
+        def quantised(name, width):
+            return sb([P, width], U32, name + "_codes"), sb([P, width], U8, name + "_scales")
+
+        def quantise(dst, src, lo, hi):
+            nc.vector.quantize_mx(
+                out=dst[0][:, lo:hi].bitcast(FP8X4), scales=dst[1][:, lo:hi], in_=src[:, PACK * lo : PACK * hi]
+            )
+
+        w3, w2, w1 = woven("w3"), woven("w2"), woven("w1")
+        q3, q2, q1 = quantised("q3", Q), quantised("q2", Q), quantised("q1", Q)
+        flat = "p r c u j -> p (r c u j)"
+        hc = RUNS // 2
+        for r in range(PACK):
+            nc.scalar.activation(
+                out=w3[:, r, 0:hc].rearrange("p c u j -> p c j u"),
+                in_=raw3[0][:].rearrange("p j (c r u) -> p r c j u", r=PACK, u=PACK)[:, r],
+                func=ACT.Copy, scale=-1.0,
+            )
+        for r in range(PACK):
+            nc.vector.tensor_scalar(
+                out=w3[:, r, hc:RUNS].rearrange("p c u j -> p c j u"),
+                in0=raw3[1][:].rearrange("p j (c r u) -> p r c j u", r=PACK, u=PACK)[:, r],
+                scalar1=-1.0, scalar2=None, op0=ALU.mult,
+            )
+        quantise(q3, w3[:].rearrange(flat), 0, Q)
+        nc.scalar.copy(
+            out=w2[:, :, 0:hc].rearrange("p r c u j -> p r c j u"),
+            in_=raw2[0][:].rearrange("p j (c r u) -> p r c j u", r=PACK, u=PACK),
+        )
+        nc.vector.tensor_copy(
+            out=w2[:, :, hc:RUNS].rearrange("p r c u j -> p r c j u"),
+            in_=raw2[1][:].rearrange("p j (c r u) -> p r c j u", r=PACK, u=PACK),
+        )
+        quantise(q2, w2[:].rearrange(flat), 0, Q)
+        nc.scalar.copy(
+            out=w1[:, :, 0:hc].rearrange("p r c u j -> p r c j u"),
+            in_=raw1[0][:].rearrange("p j (c r u) -> p r c j u", r=PACK, u=PACK),
+        )
+        for r in range(0, PACK, 2):
+            nc.vector.tensor_copy(
+                out=w1[:, r : r + 2, hc:RUNS].rearrange("p r c u j -> p r c j u"),
+                in_=raw1[1][:].rearrange("p j (c r u) -> p r c j u", r=PACK, u=PACK)[:, r : r + 2],
+            )
+        for r in range(0, PACK, 2):
+            quantise(q1, w1[:].rearrange(flat), r * P, (r + 2) * P)
+
+        def score(dst, src, r, start, stop):
+            cols = slice(r * P, (r + 1) * P)
+            nc.tensor.matmul_mx(
+                out=dst[:], lhsT=src[0][:, cols].bitcast(FP8X4), lhsT_scale=src[1][:, cols],
+                rhs=kw[:].bitcast(FP4X4), rhs_scale=kb[:], start=start, stop=stop,
+            )
+
+        tanhs = []
+        diffs = [bank("ring_a") for r in range(PACK)]
+        for r in range(PACK):
+            score(diffs[r], q3, r, True, False)
+        for r in range(PACK):
+            diff = diffs[r]
+            score(diff, q2, r, False, True)
+            th = sb([P, I], F32, "tanh%d" % r)
+            nc.scalar.activation(out=th[:], in_=diff[:], func=ACT.Tanh, scale=0.5)
+            tanhs.append(th)
+
+        a_banks, nb3_banks = [], []
+        for r in range(PACK):
+            a_banks.append(bank("ring_a"))
+            score(a_banks[r], q1, r, True, True)
+            nb3_banks.append(bank("ring_b"))
+            score(nb3_banks[r], q3, r, True, True)
+
+        turned = bank("ring_a")
+        nc.tensor.transpose(turned[:, 0:P], rows[:], ident[:])
+        gate_cols = sb([P, 2 * PACK], F32, "gate_cols")
+        nc.scalar.activation(out=gate_cols[:], in_=turned[:, ROW_EAGER : ROW_EAGER + 2 * PACK], func=ACT.Copy, scale=-0.5)
+        mean_cols = sb([P, PACK], F32, "mean_cols")
+        nc.scalar.activation(out=mean_cols[:], in_=turned[:, ROW_EAGER : ROW_EAGER + PACK], func=ACT.Copy, scale=-0.5 / I)
+        half_qs = sb([P, PACK], F32, "half_qs")
+        nc.scalar.activation(out=half_qs[:], in_=turned[:, ROW_QS : ROW_QS + PACK], func=ACT.Copy, scale=0.5)
+
+        planes = sb([P, PACK, I], BF16, "planes")
+        twice, scores, shares = {}, {}, {}
+        neg_max, gate_bias = {}, {}
+
+        def product(r):
+            twice[r] = sb([P, I], F32, "twice%d" % r)
+            nc.vector.scalar_tensor_tensor(
+                out=twice[r][:], in0=tanhs[r][:], scalar=1.0, in1=a_banks[r][:], op0=ALU.add, op1=ALU.mult
+            )
+
+        def total(r):
+            scores[r] = sb([P, I], F32, "s%d" % r)
+            s_sum = sb([P, 1], F32, "s_sum%d" % r)
+            nc.vector.scalar_tensor_tensor(
+                out=scores[r][:], in0=twice[r][:], scalar=0.5, in1=nb3_banks[r][:], op0=ALU.mult, op1=ALU.subtract,
+                accum_out=s_sum[:],
+            )
+            gate_bias[r] = sb([P, 1], F32, "gate_bias%d" % r)
+            nc.scalar.activation(
+                out=gate_bias[r][:], in_=s_sum[:], func=ACT.Identity, scale=mean_cols[:, r : r + 1],
+                bias=gate_cols[:, PACK + r : PACK + r + 1],
+            )
+
+        def softmax(r):
+            neg_max[r] = sb([P, 1], F32, "neg_max%d" % r)
+            nc.vector.tensor_reduce(out=neg_max[r][:], in_=scores[r][:], axis=AX.X, op=ALU.max, negate=True)
+            gate = sb([P, 1], F32, "gate%d" % r)
+            nc.scalar.activation(
+                out=gate[:], in_=neg_max[r][:], func=ACT.Tanh, scale=gate_cols[:, r : r + 1], bias=gate_bias[r][:]
+            )
+            p = sb([P, I], F32, "p%d" % r)
+            p_sum = sb([P, 1], F32, "p_sum%d" % r)
+            nc.scalar.activation(out=p[:], in_=scores[r][:], func=ACT.Exp, bias=neg_max[r][:], accum_out=p_sum[:])
+            gq = sb([P, 1], F32, "gq%d" % r)
+            nc.scalar.activation(
+                out=gq[:], in_=gate[:], func=ACT.Identity, scale=half_qs[:, r : r + 1], bias=half_qs[:, r : r + 1]
+            )
+            shares[r] = (p, p_sum, gq)
+
+        def weights(r):
+            p, p_sum, gq = shares[r]
+            inv = sb([P, 1], F32, "inv%d" % r)
+            nc.vector.reciprocal(out=inv[:], in_=p_sum[:])
+            if r < PACK - 1:
+                factor = sb([P, 1], F32, "factor%d" % r)
+                nc.scalar.activation(out=factor[:], in_=inv[:], func=ACT.Copy, scale=gq[:])
+                nc.scalar.activation(out=planes[:, r, :], in_=p[:], func=ACT.Copy, scale=factor[:])
+            else:
+                nc.vector.tensor_scalar(
+                    out=planes[:, r, :], in0=p[:], scalar1=inv[:], scalar2=gq[:], op0=ALU.mult, op1=ALU.mult
+                )
+
+        wm = sb([P, E, PACK], BF16, "wm")
+        qm = quantised("qm", E)
+        for k in range(E // P):
+            cols = slice(k * P, (k + 1) * P)
+            nc.scalar.copy(
+                out=wm[:, cols, :].rearrange("p (c i) r -> p c r i", i=PACK),
+                in_=raw_m[:, :, cols].rearrange("p r (c i) -> p c r i", i=PACK),
+            )
+
+        def fading(dst, k):
+            for b in range(M // BANK):
+                bs = slice(b * BANK, (b + 1) * BANK)
+                nc.gpsimd.tensor_tensor(
+                    out=dst[:, bs], in0=olds[k][:, bs],
+                    in1=fade_rows[:].rearrange("x p j -> x (p j)")[:, bs], op=ALU.mult,
+                )
+
+        early = sb([P, 2, M], F32, "faded_early")
+        fading(early[:, 0, :], 0)
+        fading(early[:, 1, :], 1)
+
+        stages = (product, total, softmax, weights)
+        for step in range(PACK + len(stages) - 1):
+            if step == PACK + 1:
+                quantise(qm, wm[:].rearrange("p e r -> p (e r)"), 0, E)
+            for lag, stage in enumerate(stages):
+                if 0 <= step - lag < PACK:
+                    stage(step - lag)
+
+        ww = sb([P, I, PACK], BF16, "ww")
+        qw = quantised("qw", I)
+        hi = I // 2
+        for h in range(2):
+            cols = slice(h * hi, (h + 1) * hi)
+            nc.vector.tensor_copy(
+                out=ww[:, cols, :].rearrange("p (c i) r -> p c r i", i=PACK),
+                in_=planes[:, :, cols].rearrange("p r (c i) -> p c r i", i=PACK),
+            )
+            quantise(qw, ww[:].rearrange("p i r -> p (i r)"), h * hi, (h + 1) * hi)
+
+        late = keep.tile([P, 2, M], F32, name="faded_late", tag="ww", align_bytes=64)
+        fading(late[:, 0, :], 2)
+        fading(late[:, 1, :], 3)
+        faded = [early[:, 0, :], early[:, 1, :], late[:, 0, :], late[:, 1, :]]
+
+        sums = []
+        for k in range(E // P):
+            cols = slice(k * P, (k + 1) * P)
+            dl_bank = bank("ring_b")
+            dl = sb([P, I], F32, "dl%d" % k)
+            parts = 2 if k == 0 else 1
+            n = I // parts
+            for h in range(parts):
+                hs = slice(h * n, (h + 1) * n)
+                nc.tensor.matmul_mx(
+                    out=dl_bank[:, hs], lhsT=qm[0][:, cols].bitcast(FP8X4), lhsT_scale=qm[1][:, cols],
+                    rhs=qw[0][:, hs].bitcast(FP8X4), rhs_scale=qw[1][:, hs], start=True, stop=True,
+                )
+                nc.scalar.copy(out=dl[:, hs], in_=dl_bank[:, hs])
+            sums.append((dl, parts, n))
+
+        for k in range(E // P):
+            dl, parts, n = sums[k]
+            window = windows[k]
+            es = slice(k * P, (k + 1) * P)
+            for h in range(parts):
+                nc.vector.tensor_copy(
+                    window[:].indirect(slot_list[:, h * n // 16 : (h + 1) * n // 16]), dl[:, h * n : (h + 1) * n]
+                )
+            adder = nc.vector if k == E // P - 1 else nc.gpsimd
+            result = sb([P, M], F32, "result%d" % k)
+            for b in range(M // BANK):
+                bs = slice(b * BANK, (b + 1) * BANK)
+                adder.tensor_tensor(out=result[:, bs], in0=faded[k][:, bs], in1=window[:, bs], op=ALU.add)
+                nc.sync.dma_start(out=out[es, bs], in_=result[:, bs])

@@ -32,7 +32,7 @@ def tile_attend_threeviews_abstaining_delivered_kernel(
     with ExitStack() as ctx:
         keep = ctx.enter_context(tc.tile_pool(name="keep", bufs=1))
         ring = ctx.enter_context(tc.tile_pool(name="ring", bufs=2))
-        psum = ctx.enter_context(tc.psum_pool(name="psum", bufs=4))
+        psum = ctx.enter_context(tc.psum_pool(name="psum", bufs=2))
 
         def sb(shape, dtype, name):
             return keep.tile(shape, dtype, name=name, align_bytes=64)
@@ -44,15 +44,14 @@ def tile_attend_threeviews_abstaining_delivered_kernel(
         nc.gpsimd.memset(key_bytes[:].bitcast(I32), 0)
         rows = sb([P, P], F32, "rows")
         nc.vector.memset(rows[:], 0.0)
-        windows = [sb([P, M], F32, "window%d" % w) for w in range(E // P)]
-        for w in windows[:2]:
+        windows = [sb([P, M], F32, "window%d" % w) for w in range(E // P + 1)]
+        for w in windows[:3]:
             nc.vector.memset(w[:], 0.0)
         ident = sb([P, P], F32, "ident")
         make_identity(nc, ident[:])
-        for w in windows[2:]:
+        for w in windows[3:]:
             nc.gpsimd.memset(w[:], 0.0)
 
-        half = Q // 2
         key_list = keep.tile([P, I // 16], U16, name="key_list")
         nc.sync.dma_start(key_list[:], offs)
         key_words = sb([P, T], U16, "key_words")
@@ -64,24 +63,19 @@ def tile_attend_threeviews_abstaining_delivered_kernel(
             )
         fade_cols = sb([P, M // P], F32, "fade_cols")
         nc.sync.dma_start(out=fade_cols[:], in_=fade.rearrange("o (p j) -> (o p) j", p=P))
-        raw3, raw2, raw1 = [], [], []
-        for src, dst, name in ((query3, raw3, "raw3"), (query2, raw2, "raw2"), (query, raw1, "raw1")):
-            for h in range(2):
-                t = sb([P, PACK, half], F32, "%s_%d" % (name, h))
-                nc.sync.dma_start(
-                    out=t[:], in_=src.rearrange("(p j) q -> p j q", j=PACK)[:, :, h * half : (h + 1) * half]
-                )
-                dst.append(t)
+        raw3, raw2, raw1 = [sb([P, PACK, Q], F32, name) for name in ("raw3", "raw2", "raw1")]
+        for src, dst in ((query3, raw3), (query2, raw2), (query, raw1)):
+            nc.sync.dma_start(out=dst[:], in_=src.rearrange("(p j) q -> p j q", j=PACK))
         for vec, row in ((eager, ROW_EAGER), (thresh, ROW_THRESH), (qs, ROW_QS)):
             nc.sync.dma_start(
                 out=rows[row : row + PACK, :].rearrange("r (c u) -> r c u", u=PACK),
                 in_=vec.rearrange("(c r u) o -> r c (u o)", r=PACK, u=PACK),
             )
         raw_m = sb([P, PACK, E], F32, "raw_m")
-        for u in range(PACK):
+        for r in range(PACK):
             nc.sync.dma_start(
-                out=raw_m[u:P:PACK, :, :],
-                in_=msgs.rearrange("(c r u) e -> u c r e", r=PACK, u=PACK)[u],
+                out=raw_m[:, r, :],
+                in_=msgs.rearrange("(c r u) e -> r c u e", r=PACK, u=PACK)[r],
             )
         olds = []
         for k in range(E // P):
@@ -96,7 +90,7 @@ def tile_attend_threeviews_abstaining_delivered_kernel(
 
         fade_rows = sb([P, P, M // P], F32, "fade_rows")
         for b in range(2):
-            fb = bank("ring_b")
+            fb = bank("pair_c")
             for jj in range(4):
                 j = 4 * b + jj
                 nc.tensor.transpose(fb[:, jj * P : (jj + 1) * P], fade_cols[:, j : j + 1].to_broadcast([P, P]), ident[:])
@@ -121,40 +115,31 @@ def tile_attend_threeviews_abstaining_delivered_kernel(
         w3, w2, w1 = woven("w3"), woven("w2"), woven("w1")
         q3, q2, q1 = quantised("q3", Q), quantised("q2", Q), quantised("q1", Q)
         flat = "p r c u j -> p (r c u j)"
-        hc = RUNS // 2
-        for r in range(PACK):
+
+        def dealt(raw):
+            return raw[:].rearrange("p j (c r u) -> p r c j u", r=PACK, u=PACK)
+
+        def weave_scalar(dst, raw, r, sign):
             nc.scalar.activation(
-                out=w3[:, r, 0:hc].rearrange("p c u j -> p c j u"),
-                in_=raw3[0][:].rearrange("p j (c r u) -> p r c j u", r=PACK, u=PACK)[:, r],
-                func=ACT.Copy, scale=-1.0,
+                out=dst[:, r].rearrange("p c u j -> p c j u"), in_=dealt(raw)[:, r], func=ACT.Copy, scale=sign
             )
-        for r in range(PACK):
+
+        def weave_vector(dst, raw, r, sign):
             nc.vector.tensor_scalar(
-                out=w3[:, r, hc:RUNS].rearrange("p c u j -> p c j u"),
-                in0=raw3[1][:].rearrange("p j (c r u) -> p r c j u", r=PACK, u=PACK)[:, r],
-                scalar1=-1.0, scalar2=None, op0=ALU.mult,
+                out=dst[:, r].rearrange("p c u j -> p c j u"), in0=dealt(raw)[:, r],
+                scalar1=sign, scalar2=None, op0=ALU.mult,
             )
-        quantise(q3, w3[:].rearrange(flat), 0, Q)
-        nc.scalar.copy(
-            out=w2[:, :, 0:hc].rearrange("p r c u j -> p r c j u"),
-            in_=raw2[0][:].rearrange("p j (c r u) -> p r c j u", r=PACK, u=PACK),
-        )
-        nc.vector.tensor_copy(
-            out=w2[:, :, hc:RUNS].rearrange("p r c u j -> p r c j u"),
-            in_=raw2[1][:].rearrange("p j (c r u) -> p r c j u", r=PACK, u=PACK),
-        )
-        quantise(q2, w2[:].rearrange(flat), 0, Q)
-        nc.scalar.copy(
-            out=w1[:, :, 0:hc].rearrange("p r c u j -> p r c j u"),
-            in_=raw1[0][:].rearrange("p j (c r u) -> p r c j u", r=PACK, u=PACK),
-        )
-        for r in range(0, PACK, 2):
-            nc.vector.tensor_copy(
-                out=w1[:, r : r + 2, hc:RUNS].rearrange("p r c u j -> p r c j u"),
-                in_=raw1[1][:].rearrange("p j (c r u) -> p r c j u", r=PACK, u=PACK)[:, r : r + 2],
-            )
-        for r in range(0, PACK, 2):
-            quantise(q1, w1[:].rearrange(flat), r * P, (r + 2) * P)
+
+        for dst, raw, codes, sign in ((w3, raw3, q3, -1.0), (w2, raw2, q2, 1.0)):
+            for r in (2, 3):
+                weave_scalar(dst, raw, r, sign)
+            for r in (0, 1):
+                weave_vector(dst, raw, r, sign)
+            for r in (0, 2):
+                quantise(codes, dst[:].rearrange(flat), r * P, (r + 2) * P)
+        for r in (0, 1):
+            weave_vector(w1, raw1, r, 1.0)
+        quantise(q1, w1[:].rearrange(flat), 0, 2 * P)
 
         def score(dst, src, r, start, stop):
             cols = slice(r * P, (r + 1) * P)
@@ -164,7 +149,7 @@ def tile_attend_threeviews_abstaining_delivered_kernel(
             )
 
         tanhs = []
-        diffs = [bank("ring_a") for r in range(PACK)]
+        diffs = [bank(("pair_a", "pair_b")[r % 2]) for r in range(PACK)]
         for r in range(PACK):
             score(diffs[r], q3, r, True, False)
         for r in range(PACK):
@@ -173,15 +158,18 @@ def tile_attend_threeviews_abstaining_delivered_kernel(
             th = sb([P, I], F32, "tanh%d" % r)
             nc.scalar.activation(out=th[:], in_=diff[:], func=ACT.Tanh, scale=0.5)
             tanhs.append(th)
+            if r < 2:
+                weave_scalar(w1, raw1, r + 2, 1.0)
+        quantise(q1, w1[:].rearrange(flat), 2 * P, Q)
 
         a_banks, nb3_banks = [], []
         for r in range(PACK):
-            a_banks.append(bank("ring_a"))
+            a_banks.append(bank(("pair_a", "pair_b")[r % 2]))
             score(a_banks[r], q1, r, True, True)
-            nb3_banks.append(bank("ring_b"))
+            nb3_banks.append(bank(("pair_c", "pair_d")[r % 2]))
             score(nb3_banks[r], q3, r, True, True)
 
-        turned = bank("ring_a")
+        turned = bank("pair_a")
         nc.tensor.transpose(turned[:, 0:P], rows[:], ident[:])
         gate_cols = sb([P, 2 * PACK], F32, "gate_cols")
         nc.scalar.activation(out=gate_cols[:], in_=turned[:, ROW_EAGER : ROW_EAGER + 2 * PACK], func=ACT.Copy, scale=-0.5)
@@ -259,9 +247,9 @@ def tile_attend_threeviews_abstaining_delivered_kernel(
                     in1=fade_rows[:].rearrange("x p j -> x (p j)")[:, bs], op=ALU.mult,
                 )
 
-        early = sb([P, 2, M], F32, "faded_early")
-        fading(early[:, 0, :], 0)
-        fading(early[:, 1, :], 1)
+        faded = [sb([P, M], F32, "faded%d" % k) for k in range(E // P - 1)]
+        for k in range(E // P - 1):
+            fading(faded[k], k)
 
         stages = (product, total, softmax, weights)
         for step in range(PACK + len(stages) - 1):
@@ -282,38 +270,63 @@ def tile_attend_threeviews_abstaining_delivered_kernel(
             )
             quantise(qw, ww[:].rearrange("p i r -> p (i r)"), h * hi, (h + 1) * hi)
 
-        late = keep.tile([P, 2, M], F32, name="faded_late", tag="ww", align_bytes=64)
-        fading(late[:, 0, :], 2)
-        fading(late[:, 1, :], 3)
-        faded = [early[:, 0, :], early[:, 1, :], late[:, 0, :], late[:, 1, :]]
+        late = keep.tile([P, M], F32, name="faded_late", tag="ww", align_bytes=64)
+        fading(late, E // P - 1)
+        faded.append(late)
 
-        sums = []
-        for k in range(E // P):
+        def deliver(k, lo, hi, pair, window):
             cols = slice(k * P, (k + 1) * P)
-            dl_bank = bank("ring_b")
-            dl = sb([P, I], F32, "dl%d" % k)
-            parts = 2 if k == 0 else 1
-            n = I // parts
-            for h in range(parts):
-                hs = slice(h * n, (h + 1) * n)
-                nc.tensor.matmul_mx(
-                    out=dl_bank[:, hs], lhsT=qm[0][:, cols].bitcast(FP8X4), lhsT_scale=qm[1][:, cols],
-                    rhs=qw[0][:, hs].bitcast(FP8X4), rhs_scale=qw[1][:, hs], start=True, stop=True,
+            dl_bank = bank(pair)
+            nc.tensor.matmul_mx(
+                out=dl_bank[:, 0 : hi - lo], lhsT=qm[0][:, cols].bitcast(FP8X4), lhsT_scale=qm[1][:, cols],
+                rhs=qw[0][:, lo:hi].bitcast(FP8X4), rhs_scale=qw[1][:, lo:hi], start=True, stop=True,
+            )
+            dl = sb([P, hi - lo], F32, "dl%d_%d" % (k, lo))
+            nc.scalar.copy(out=dl[:], in_=dl_bank[:, 0 : hi - lo])
+            nc.vector.tensor_copy(window[:].indirect(slot_list[:, lo // 16 : hi // 16]), dl[:])
+
+        per_bank = BANK // P
+
+        def turn(dst, src, b, start, stop):
+            for jj in range(per_bank):
+                j = b * per_bank + jj
+                nc.tensor.matmul(
+                    dst[:, jj * P : (jj + 1) * P], src[:, j * P : (j + 1) * P], ident[:],
+                    start=start and jj == 0, stop=stop and jj == per_bank - 1, is_transpose=True,
                 )
-                nc.scalar.copy(out=dl[:, hs], in_=dl_bank[:, hs])
-            sums.append((dl, parts, n))
 
         for k in range(E // P):
-            dl, parts, n = sums[k]
             window = windows[k]
             es = slice(k * P, (k + 1) * P)
-            for h in range(parts):
-                nc.vector.tensor_copy(
-                    window[:].indirect(slot_list[:, h * n // 16 : (h + 1) * n // 16]), dl[:, h * n : (h + 1) * n]
-                )
-            adder = nc.vector if k == E // P - 1 else nc.gpsimd
+            last = k == E // P - 1
+            sum_banks = []
+            if not last:
+                for b in range(M // BANK):
+                    sum_banks.append(bank("pair_c"))
+                    turn(sum_banks[b], faded[k], b, True, False)
+            if k == 0:
+                deliver(k, 0, hi, "pair_a", windows[E // P])
+                for b in range(M // BANK):
+                    turn(sum_banks[b], windows[E // P], b, False, False)
+                deliver(k, hi, I, "pair_b", window)
+            else:
+                deliver(k, 0, I, ("pair_b", "pair_a")[k % 2], window)
             result = sb([P, M], F32, "result%d" % k)
-            for b in range(M // BANK):
-                bs = slice(b * BANK, (b + 1) * BANK)
-                adder.tensor_tensor(out=result[:, bs], in0=faded[k][:, bs], in1=window[:, bs], op=ALU.add)
-                nc.sync.dma_start(out=out[es, bs], in_=result[:, bs])
+            if last:
+                for b in range(M // BANK):
+                    bs = slice(b * BANK, (b + 1) * BANK)
+                    nc.vector.tensor_tensor(out=result[:, bs], in0=faded[k][:, bs], in1=window[:, bs], op=ALU.add)
+                    nc.sync.dma_start(out=out[es, bs], in_=result[:, bs])
+            else:
+                turned_sum = ring.tile([P, M], F32, name="turned_sum")
+                for b in range(M // BANK):
+                    turn(sum_banks[b], window, b, False, True)
+                    nc.scalar.copy(out=turned_sum[:, b * BANK : (b + 1) * BANK], in_=sum_banks[b][:])
+                for b in range(M // BANK):
+                    bs = slice(b * BANK, (b + 1) * BANK)
+                    back = bank("pair_d")
+                    for jj in range(per_bank):
+                        j = b * per_bank + jj
+                        nc.tensor.transpose(back[:, jj * P : (jj + 1) * P], turned_sum[:, j * P : (j + 1) * P], ident[:])
+                    nc.scalar.copy(out=result[:, bs], in_=back[:])
+                    nc.scalar.dma_start(out=out[es, bs], in_=result[:, bs])

@@ -22,7 +22,7 @@ P = 128
 PACK = 4
 RUNS = 32
 BANK = 512
-ROW_EAGER, ROW_THRESH, ROW_QS, ROW_FADE = 0, 4, 8, 16
+ROW_EAGER, ROW_THRESH, ROW_QS = 0, 1, 2
 
 
 def tile_attend_threeviews_abstaining_delivered_kernel(
@@ -42,7 +42,7 @@ def tile_attend_threeviews_abstaining_delivered_kernel(
 
         key_bytes = sb([P, T], U8, "key_bytes")
         nc.gpsimd.memset(key_bytes[:].bitcast(I32), 0)
-        rows = sb([P, P], F32, "rows")
+        rows = sb([P, Q], F32, "rows")
         nc.vector.memset(rows[:], 0.0)
         windows = [sb([P, M], F32, "window%d" % w) for w in range(E // P + 1)]
         for w in windows[:3]:
@@ -64,13 +64,11 @@ def tile_attend_threeviews_abstaining_delivered_kernel(
         fade_cols = sb([P, M // P], F32, "fade_cols")
         nc.sync.dma_start(out=fade_cols[:], in_=fade.rearrange("o (p j) -> (o p) j", p=P))
         raw3, raw2, raw1 = [sb([P, PACK, Q], F32, name) for name in ("raw3", "raw2", "raw1")]
-        for src, dst in ((query3, raw3), (query2, raw2), (query, raw1)):
+        for src, dst in ((query3, raw3), (query2, raw2)):
             nc.sync.dma_start(out=dst[:], in_=src.rearrange("(p j) q -> p j q", j=PACK))
         for vec, row in ((eager, ROW_EAGER), (thresh, ROW_THRESH), (qs, ROW_QS)):
-            nc.sync.dma_start(
-                out=rows[row : row + PACK, :].rearrange("r (c u) -> r c u", u=PACK),
-                in_=vec.rearrange("(c r u) o -> r c (u o)", r=PACK, u=PACK),
-            )
+            nc.sync.dma_start(out=rows[row : row + 1, :], in_=vec.rearrange("q o -> o q"))
+        nc.sync.dma_start(out=raw1[:], in_=query.rearrange("(p j) q -> p j q", j=PACK))
         raw_m = sb([P, PACK, E], F32, "raw_m")
         for r in range(PACK):
             nc.sync.dma_start(
@@ -86,7 +84,7 @@ def tile_attend_threeviews_abstaining_delivered_kernel(
         nc.sync.dma_start(slot_list[:], offs2)
 
         warm = sb([P, 1], F32, "warm")
-        nc.scalar.activation(out=warm[:], in_=rows[:, P - 1 : P], func=ACT.Tanh)
+        nc.scalar.activation(out=warm[:], in_=rows[:, 0:1], func=ACT.Tanh)
 
         fade_rows = sb([P, P, M // P], F32, "fade_rows")
         for b in range(2):
@@ -141,6 +139,9 @@ def tile_attend_threeviews_abstaining_delivered_kernel(
             weave_vector(w1, raw1, r, 1.0)
         quantise(q1, w1[:].rearrange(flat), 0, 2 * P)
 
+        dealt_rows = sb([P, PACK, RUNS, PACK], F32, "dealt_rows")
+        nc.scalar.copy(out=dealt_rows[:], in_=rows[:].rearrange("v (c r u) -> v r c u", r=PACK, u=PACK))
+
         def score(dst, src, r, start, stop):
             cols = slice(r * P, (r + 1) * P)
             nc.tensor.matmul_mx(
@@ -170,13 +171,20 @@ def tile_attend_threeviews_abstaining_delivered_kernel(
             score(nb3_banks[r], q3, r, True, True)
 
         turned = bank("pair_a")
-        nc.tensor.transpose(turned[:, 0:P], rows[:], ident[:])
-        gate_cols = sb([P, 2 * PACK], F32, "gate_cols")
-        nc.scalar.activation(out=gate_cols[:], in_=turned[:, ROW_EAGER : ROW_EAGER + 2 * PACK], func=ACT.Copy, scale=-0.5)
-        mean_cols = sb([P, PACK], F32, "mean_cols")
-        nc.scalar.activation(out=mean_cols[:], in_=turned[:, ROW_EAGER : ROW_EAGER + PACK], func=ACT.Copy, scale=-0.5 / I)
-        half_qs = sb([P, PACK], F32, "half_qs")
-        nc.scalar.activation(out=half_qs[:], in_=turned[:, ROW_QS : ROW_QS + PACK], func=ACT.Copy, scale=0.5)
+        for r in range(PACK):
+            nc.tensor.transpose(
+                turned[:, r * P : (r + 1) * P], dealt_rows[:, r].rearrange("v c u -> v (c u)"), ident[:]
+            )
+
+        def columns(name, row, scale):
+            t = sb([P, PACK], F32, name)
+            nc.scalar.activation(out=t[:], in_=turned[:, row:BANK:P], func=ACT.Copy, scale=scale)
+            return t
+
+        mean_cols = columns("mean_cols", ROW_EAGER, -0.5 / I)
+        thresh_cols = columns("thresh_cols", ROW_THRESH, -0.5)
+        eager_cols = columns("eager_cols", ROW_EAGER, -0.5)
+        half_qs = columns("half_qs", ROW_QS, 0.5)
 
         planes = sb([P, PACK, I], BF16, "planes")
         twice, scores, shares = {}, {}, {}
@@ -198,7 +206,7 @@ def tile_attend_threeviews_abstaining_delivered_kernel(
             gate_bias[r] = sb([P, 1], F32, "gate_bias%d" % r)
             nc.scalar.activation(
                 out=gate_bias[r][:], in_=s_sum[:], func=ACT.Identity, scale=mean_cols[:, r : r + 1],
-                bias=gate_cols[:, PACK + r : PACK + r + 1],
+                bias=thresh_cols[:, r : r + 1],
             )
 
         def softmax(r):
@@ -206,7 +214,7 @@ def tile_attend_threeviews_abstaining_delivered_kernel(
             nc.vector.tensor_reduce(out=neg_max[r][:], in_=scores[r][:], axis=AX.X, op=ALU.max, negate=True)
             gate = sb([P, 1], F32, "gate%d" % r)
             nc.scalar.activation(
-                out=gate[:], in_=neg_max[r][:], func=ACT.Tanh, scale=gate_cols[:, r : r + 1], bias=gate_bias[r][:]
+                out=gate[:], in_=neg_max[r][:], func=ACT.Tanh, scale=eager_cols[:, r : r + 1], bias=gate_bias[r][:]
             )
             p = sb([P, I], F32, "p%d" % r)
             p_sum = sb([P, 1], F32, "p_sum%d" % r)
@@ -234,9 +242,9 @@ def tile_attend_threeviews_abstaining_delivered_kernel(
         qm = quantised("qm", E)
         for k in range(E // P):
             cols = slice(k * P, (k + 1) * P)
-            nc.scalar.copy(
-                out=wm[:, cols, :].rearrange("p (c i) r -> p c r i", i=PACK),
-                in_=raw_m[:, :, cols].rearrange("p r (c i) -> p c r i", i=PACK),
+            nc.gpsimd.tensor_scalar(
+                out=wm[:, cols, :], in0=raw_m[:, :, cols].rearrange("p r e -> p e r"),
+                scalar1=1.0, scalar2=0.0, op0=ALU.mult, op1=ALU.add,
             )
 
         def fading(dst, k):
@@ -247,8 +255,8 @@ def tile_attend_threeviews_abstaining_delivered_kernel(
                     in1=fade_rows[:].rearrange("x p j -> x (p j)")[:, bs], op=ALU.mult,
                 )
 
-        faded = [sb([P, M], F32, "faded%d" % k) for k in range(E // P - 1)]
-        for k in range(E // P - 1):
+        faded = [sb([P, M], F32, "faded%d" % k)[:] for k in range(2)]
+        for k in range(2):
             fading(faded[k], k)
 
         stages = (product, total, softmax, weights)
@@ -262,17 +270,18 @@ def tile_attend_threeviews_abstaining_delivered_kernel(
         ww = sb([P, I, PACK], BF16, "ww")
         qw = quantised("qw", I)
         hi = I // 2
-        for h in range(2):
-            cols = slice(h * hi, (h + 1) * hi)
+        for h in range(I // P):
+            cols = slice(h * P, (h + 1) * P)
             nc.vector.tensor_copy(
                 out=ww[:, cols, :].rearrange("p (c i) r -> p c r i", i=PACK),
                 in_=planes[:, :, cols].rearrange("p r (c i) -> p c r i", i=PACK),
             )
-            quantise(qw, ww[:].rearrange("p i r -> p (i r)"), h * hi, (h + 1) * hi)
+            quantise(qw, ww[:].rearrange("p i r -> p (i r)"), h * P, (h + 1) * P)
 
-        late = keep.tile([P, M], F32, name="faded_late", tag="ww", align_bytes=64)
-        fading(late, E // P - 1)
-        faded.append(late)
+        late = keep.tile([P, 2, M], F32, name="faded_late", tag="ww", align_bytes=64)
+        for k in range(2, E // P):
+            faded.append(late[:, k - 2, :])
+            fading(faded[k], k)
 
         def deliver(k, lo, hi, pair, window):
             cols = slice(k * P, (k + 1) * P)

@@ -165,9 +165,9 @@ def tile_attend_threeviews_abstaining_delivered_kernel(
 
         a_banks, nb3_banks = [], []
         for r in range(PACK):
-            a_banks.append(bank(("pair_a", "pair_b")[r % 2]))
+            a_banks.append(bank(("pair_c", "pair_d")[r % 2]))
             score(a_banks[r], q1, r, True, True)
-            nb3_banks.append(bank(("pair_c", "pair_d")[r % 2]))
+            nb3_banks.append(bank(("pair_a", "pair_b")[r % 2]))
             score(nb3_banks[r], q3, r, True, True)
 
         turned = bank("pair_a")
@@ -259,13 +259,13 @@ def tile_attend_threeviews_abstaining_delivered_kernel(
         for k in range(2):
             fading(faded[k], k)
 
-        stages = (product, total, softmax, weights)
-        for step in range(PACK + len(stages) - 1):
-            if step == PACK + 1:
+        for r in range(PACK):
+            product(r)
+            total(r)
+            softmax(r)
+            if r == PACK - 1:
                 quantise(qm, wm[:].rearrange("p e r -> p (e r)"), 0, E)
-            for lag, stage in enumerate(stages):
-                if 0 <= step - lag < PACK:
-                    stage(step - lag)
+            weights(r)
 
         ww = sb([P, I, PACK], BF16, "ww")
         qw = quantised("qw", I)

@@ -20,9 +20,17 @@ AX = mybir.AxisListType
 
 P = 128
 PACK = 4
-RUNS = 32
+RUNS = P // PACK
 BANK = 512
+BLOCKS = BANK // P
+HALVES = M // BANK
+E_TILES = E // P
+LIST_ROWS = 16
+QUADS, QUAD_ROWS, SCALE_ROWS = 4, 32, 4
 ROW_EAGER, ROW_THRESH, ROW_QS = 0, 1, 2
+VECTOR_TILES, SCALAR_TILES = (0, 1), (2, 3)
+VECTOR_CLEARS = 3
+EARLY_FADED = 2
 
 
 def tile_attend_threeviews_abstaining_delivered_kernel(
@@ -44,22 +52,22 @@ def tile_attend_threeviews_abstaining_delivered_kernel(
         nc.gpsimd.memset(key_bytes[:].bitcast(I32), 0)
         rows = sb([P, Q], F32, "rows")
         nc.vector.memset(rows[:], 0.0)
-        windows = [sb([P, M], F32, "window%d" % w) for w in range(E // P + 1)]
-        for w in windows[:3]:
+        windows = [sb([P, M], F32, "window%d" % w) for w in range(E_TILES + 1)]
+        for w in windows[:VECTOR_CLEARS]:
             nc.vector.memset(w[:], 0.0)
         ident = sb([P, P], F32, "ident")
         make_identity(nc, ident[:])
-        for w in windows[3:]:
+        for w in windows[VECTOR_CLEARS:]:
             nc.gpsimd.memset(w[:], 0.0)
 
-        key_list = keep.tile([P, I // 16], U16, name="key_list")
+        key_list = keep.tile([P, I // LIST_ROWS], U16, name="key_list")
         nc.sync.dma_start(key_list[:], offs)
         key_words = sb([P, T], U16, "key_words")
         nc.sync.dma_start(out=key_words[:].bitcast(I32), in_=keys_words[0].bitcast(I32))
-        for quad in range(4):
+        for quad in range(QUADS):
             nc.sync.dma_start(
-                out=key_bytes[32 * quad : 32 * quad + 4, :].bitcast(I32),
-                in_=keys_scales[0, 4 * quad : 4 * quad + 4, :].bitcast(I32),
+                out=key_bytes[QUAD_ROWS * quad : QUAD_ROWS * quad + SCALE_ROWS, :].bitcast(I32),
+                in_=keys_scales[0, SCALE_ROWS * quad : SCALE_ROWS * (quad + 1), :].bitcast(I32),
             )
         fade_cols = sb([P, M // P], F32, "fade_cols")
         nc.sync.dma_start(out=fade_cols[:], in_=fade.rearrange("o (p j) -> (o p) j", p=P))
@@ -76,23 +84,24 @@ def tile_attend_threeviews_abstaining_delivered_kernel(
                 in_=msgs.rearrange("(c r u) e -> r c u e", r=PACK, u=PACK)[r],
             )
         olds = []
-        for k in range(E // P):
-            t = sb([P, M], F32, "old%d" % k)
-            nc.sync.dma_start(out=t[:], in_=old[k * P : (k + 1) * P, :])
-            olds.append(t)
-        slot_list = keep.tile([P, I // 16], U16, name="slot_list")
+        for k in range(E_TILES):
+            old_tile = sb([P, M], F32, "old%d" % k)
+            nc.sync.dma_start(out=old_tile[:], in_=old[k * P : (k + 1) * P, :])
+            olds.append(old_tile)
+        slot_list = keep.tile([P, I // LIST_ROWS], U16, name="slot_list")
         nc.sync.dma_start(slot_list[:], offs2)
 
-        warm = sb([P, 1], F32, "warm")
-        nc.scalar.activation(out=warm[:], in_=rows[:, 0:1], func=ACT.Tanh)
-
         fade_rows = sb([P, P, M // P], F32, "fade_rows")
-        for b in range(2):
-            fb = bank("pair_c")
-            for jj in range(4):
-                j = 4 * b + jj
-                nc.tensor.transpose(fb[:, jj * P : (jj + 1) * P], fade_cols[:, j : j + 1].to_broadcast([P, P]), ident[:])
-            nc.scalar.copy(out=fade_rows[:, :, 4 * b : 4 * b + 4], in_=fb[:].rearrange("x (j p) -> x p j", p=P))
+        for b in range(HALVES):
+            fade_bank = bank("pair_c")
+            for jj in range(BLOCKS):
+                j = BLOCKS * b + jj
+                nc.tensor.transpose(
+                    fade_bank[:, jj * P : (jj + 1) * P], fade_cols[:, j : j + 1].to_broadcast([P, P]), ident[:]
+                )
+            nc.scalar.copy(
+                out=fade_rows[:, :, BLOCKS * b : BLOCKS * (b + 1)], in_=fade_bank[:].rearrange("x (j p) -> x p j", p=P)
+            )
 
         kw = sb([P, I], U16, "kw")
         nc.vector.tensor_copy(kw[:], key_words[:].indirect(key_list[:]))
@@ -128,16 +137,19 @@ def tile_attend_threeviews_abstaining_delivered_kernel(
                 scalar1=sign, scalar2=None, op0=ALU.mult,
             )
 
+        def quantise_tiles(codes, src, tiles):
+            quantise(codes, src[:].rearrange(flat), tiles[0] * P, (tiles[-1] + 1) * P)
+
         for dst, raw, codes, sign in ((w3, raw3, q3, -1.0), (w2, raw2, q2, 1.0)):
-            for r in (2, 3):
+            for r in SCALAR_TILES:
                 weave_scalar(dst, raw, r, sign)
-            for r in (0, 1):
+            for r in VECTOR_TILES:
                 weave_vector(dst, raw, r, sign)
-            for r in (0, 2):
-                quantise(codes, dst[:].rearrange(flat), r * P, (r + 2) * P)
-        for r in (0, 1):
+            for tiles in (VECTOR_TILES, SCALAR_TILES):
+                quantise_tiles(codes, dst, tiles)
+        for r in VECTOR_TILES:
             weave_vector(w1, raw1, r, 1.0)
-        quantise(q1, w1[:].rearrange(flat), 0, 2 * P)
+        quantise_tiles(q1, w1, VECTOR_TILES)
 
         dealt_rows = sb([P, PACK, RUNS, PACK], F32, "dealt_rows")
         nc.scalar.copy(out=dealt_rows[:], in_=rows[:].rearrange("v (c r u) -> v r c u", r=PACK, u=PACK))
@@ -154,14 +166,13 @@ def tile_attend_threeviews_abstaining_delivered_kernel(
         for r in range(PACK):
             score(diffs[r], q3, r, True, False)
         for r in range(PACK):
-            diff = diffs[r]
-            score(diff, q2, r, False, True)
+            score(diffs[r], q2, r, False, True)
             th = sb([P, I], F32, "tanh%d" % r)
-            nc.scalar.activation(out=th[:], in_=diff[:], func=ACT.Tanh, scale=0.5)
+            nc.scalar.activation(out=th[:], in_=diffs[r][:], func=ACT.Tanh, scale=0.5)
             tanhs.append(th)
-            if r < 2:
-                weave_scalar(w1, raw1, r + 2, 1.0)
-        quantise(q1, w1[:].rearrange(flat), 2 * P, Q)
+            if r < len(SCALAR_TILES):
+                weave_scalar(w1, raw1, SCALAR_TILES[r], 1.0)
+        quantise_tiles(q1, w1, SCALAR_TILES)
 
         a_banks, nb3_banks = [], []
         for r in range(PACK):
@@ -177,9 +188,9 @@ def tile_attend_threeviews_abstaining_delivered_kernel(
             )
 
         def columns(name, row, scale):
-            t = sb([P, PACK], F32, name)
-            nc.scalar.activation(out=t[:], in_=turned[:, row:BANK:P], func=ACT.Copy, scale=scale)
-            return t
+            cols_tile = sb([P, PACK], F32, name)
+            nc.scalar.activation(out=cols_tile[:], in_=turned[:, row:BANK:P], func=ACT.Copy, scale=scale)
+            return cols_tile
 
         mean_cols = columns("mean_cols", ROW_EAGER, -0.5 / I)
         thresh_cols = columns("thresh_cols", ROW_THRESH, -0.5)
@@ -187,60 +198,10 @@ def tile_attend_threeviews_abstaining_delivered_kernel(
         half_qs = columns("half_qs", ROW_QS, 0.5)
 
         planes = sb([P, PACK, I], BF16, "planes")
-        twice, scores, shares = {}, {}, {}
-        neg_max, gate_bias = {}, {}
-
-        def product(r):
-            twice[r] = sb([P, I], F32, "twice%d" % r)
-            nc.vector.scalar_tensor_tensor(
-                out=twice[r][:], in0=tanhs[r][:], scalar=1.0, in1=a_banks[r][:], op0=ALU.add, op1=ALU.mult
-            )
-
-        def total(r):
-            scores[r] = sb([P, I], F32, "s%d" % r)
-            s_sum = sb([P, 1], F32, "s_sum%d" % r)
-            nc.vector.scalar_tensor_tensor(
-                out=scores[r][:], in0=twice[r][:], scalar=0.5, in1=nb3_banks[r][:], op0=ALU.mult, op1=ALU.subtract,
-                accum_out=s_sum[:],
-            )
-            gate_bias[r] = sb([P, 1], F32, "gate_bias%d" % r)
-            nc.scalar.activation(
-                out=gate_bias[r][:], in_=s_sum[:], func=ACT.Identity, scale=mean_cols[:, r : r + 1],
-                bias=thresh_cols[:, r : r + 1],
-            )
-
-        def softmax(r):
-            neg_max[r] = sb([P, 1], F32, "neg_max%d" % r)
-            nc.vector.tensor_reduce(out=neg_max[r][:], in_=scores[r][:], axis=AX.X, op=ALU.max, negate=True)
-            gate = sb([P, 1], F32, "gate%d" % r)
-            nc.scalar.activation(
-                out=gate[:], in_=neg_max[r][:], func=ACT.Tanh, scale=eager_cols[:, r : r + 1], bias=gate_bias[r][:]
-            )
-            p = sb([P, I], F32, "p%d" % r)
-            p_sum = sb([P, 1], F32, "p_sum%d" % r)
-            nc.scalar.activation(out=p[:], in_=scores[r][:], func=ACT.Exp, bias=neg_max[r][:], accum_out=p_sum[:])
-            gq = sb([P, 1], F32, "gq%d" % r)
-            nc.scalar.activation(
-                out=gq[:], in_=gate[:], func=ACT.Identity, scale=half_qs[:, r : r + 1], bias=half_qs[:, r : r + 1]
-            )
-            shares[r] = (p, p_sum, gq)
-
-        def weights(r):
-            p, p_sum, gq = shares[r]
-            inv = sb([P, 1], F32, "inv%d" % r)
-            nc.vector.reciprocal(out=inv[:], in_=p_sum[:])
-            if r < PACK - 1:
-                factor = sb([P, 1], F32, "factor%d" % r)
-                nc.scalar.activation(out=factor[:], in_=inv[:], func=ACT.Copy, scale=gq[:])
-                nc.scalar.activation(out=planes[:, r, :], in_=p[:], func=ACT.Copy, scale=factor[:])
-            else:
-                nc.vector.tensor_scalar(
-                    out=planes[:, r, :], in0=p[:], scalar1=inv[:], scalar2=gq[:], op0=ALU.mult, op1=ALU.mult
-                )
 
         wm = sb([P, E, PACK], BF16, "wm")
         qm = quantised("qm", E)
-        for k in range(E // P):
+        for k in range(E_TILES):
             cols = slice(k * P, (k + 1) * P)
             nc.gpsimd.tensor_scalar(
                 out=wm[:, cols, :], in0=raw_m[:, :, cols].rearrange("p r e -> p e r"),
@@ -248,28 +209,62 @@ def tile_attend_threeviews_abstaining_delivered_kernel(
             )
 
         def fading(dst, k):
-            for b in range(M // BANK):
+            for b in range(HALVES):
                 bs = slice(b * BANK, (b + 1) * BANK)
                 nc.gpsimd.tensor_tensor(
                     out=dst[:, bs], in0=olds[k][:, bs],
                     in1=fade_rows[:].rearrange("x p j -> x (p j)")[:, bs], op=ALU.mult,
                 )
 
-        faded = [sb([P, M], F32, "faded%d" % k)[:] for k in range(2)]
-        for k in range(2):
+        faded = [sb([P, M], F32, "faded%d" % k)[:] for k in range(EARLY_FADED)]
+        for k in range(EARLY_FADED):
             fading(faded[k], k)
 
         for r in range(PACK):
-            product(r)
-            total(r)
-            softmax(r)
-            if r == PACK - 1:
+            col = slice(r, r + 1)
+            last_tile = r == PACK - 1
+            twice = sb([P, I], F32, "twice%d" % r)
+            nc.vector.scalar_tensor_tensor(
+                out=twice[:], in0=tanhs[r][:], scalar=1.0, in1=a_banks[r][:], op0=ALU.add, op1=ALU.mult
+            )
+            s = sb([P, I], F32, "s%d" % r)
+            s_sum = sb([P, 1], F32, "s_sum%d" % r)
+            nc.vector.scalar_tensor_tensor(
+                out=s[:], in0=twice[:], scalar=0.5, in1=nb3_banks[r][:], op0=ALU.mult, op1=ALU.subtract,
+                accum_out=s_sum[:],
+            )
+            gate_bias = sb([P, 1], F32, "gate_bias%d" % r)
+            nc.scalar.activation(
+                out=gate_bias[:], in_=s_sum[:], func=ACT.Identity, scale=mean_cols[:, col], bias=thresh_cols[:, col]
+            )
+            neg_max = sb([P, 1], F32, "neg_max%d" % r)
+            nc.vector.tensor_reduce(out=neg_max[:], in_=s[:], axis=AX.X, op=ALU.max, negate=True)
+            gate = sb([P, 1], F32, "gate%d" % r)
+            nc.scalar.activation(
+                out=gate[:], in_=neg_max[:], func=ACT.Tanh, scale=eager_cols[:, col], bias=gate_bias[:]
+            )
+            expd = sb([P, I], F32, "p%d" % r)
+            exp_sum = sb([P, 1], F32, "p_sum%d" % r)
+            nc.scalar.activation(out=expd[:], in_=s[:], func=ACT.Exp, bias=neg_max[:], accum_out=exp_sum[:])
+            gq = sb([P, 1], F32, "gq%d" % r)
+            nc.scalar.activation(
+                out=gq[:], in_=gate[:], func=ACT.Identity, scale=half_qs[:, col], bias=half_qs[:, col]
+            )
+            if last_tile:
                 quantise(qm, wm[:].rearrange("p e r -> p (e r)"), 0, E)
-            weights(r)
+            inv = sb([P, 1], F32, "inv%d" % r)
+            nc.vector.reciprocal(out=inv[:], in_=exp_sum[:])
+            if last_tile:
+                nc.vector.tensor_scalar(
+                    out=planes[:, r, :], in0=expd[:], scalar1=inv[:], scalar2=gq[:], op0=ALU.mult, op1=ALU.mult
+                )
+            else:
+                factor = sb([P, 1], F32, "factor%d" % r)
+                nc.scalar.activation(out=factor[:], in_=inv[:], func=ACT.Copy, scale=gq[:])
+                nc.scalar.activation(out=planes[:, r, :], in_=expd[:], func=ACT.Copy, scale=factor[:])
 
         ww = sb([P, I, PACK], BF16, "ww")
         qw = quantised("qw", I)
-        hi = I // 2
         for h in range(I // P):
             cols = slice(h * P, (h + 1) * P)
             nc.vector.tensor_copy(
@@ -278,9 +273,9 @@ def tile_attend_threeviews_abstaining_delivered_kernel(
             )
             quantise(qw, ww[:].rearrange("p i r -> p (i r)"), h * P, (h + 1) * P)
 
-        late = keep.tile([P, 2, M], F32, name="faded_late", tag="ww", align_bytes=64)
-        for k in range(2, E // P):
-            faded.append(late[:, k - 2, :])
+        late = keep.tile([P, E_TILES - EARLY_FADED, M], F32, name="faded_late", tag="ww", align_bytes=64)
+        for k in range(EARLY_FADED, E_TILES):
+            faded.append(late[:, k - EARLY_FADED, :])
             fading(faded[k], k)
 
         def deliver(k, lo, hi, pair, window):
@@ -292,50 +287,50 @@ def tile_attend_threeviews_abstaining_delivered_kernel(
             )
             dl = sb([P, hi - lo], F32, "dl%d_%d" % (k, lo))
             nc.scalar.copy(out=dl[:], in_=dl_bank[:, 0 : hi - lo])
-            nc.vector.tensor_copy(window[:].indirect(slot_list[:, lo // 16 : hi // 16]), dl[:])
-
-        per_bank = BANK // P
+            nc.vector.tensor_copy(window[:].indirect(slot_list[:, lo // LIST_ROWS : hi // LIST_ROWS]), dl[:])
 
         def turn(dst, src, b, start, stop):
-            for jj in range(per_bank):
-                j = b * per_bank + jj
+            for jj in range(BLOCKS):
+                j = b * BLOCKS + jj
                 nc.tensor.matmul(
                     dst[:, jj * P : (jj + 1) * P], src[:, j * P : (j + 1) * P], ident[:],
-                    start=start and jj == 0, stop=stop and jj == per_bank - 1, is_transpose=True,
+                    start=start and jj == 0, stop=stop and jj == BLOCKS - 1, is_transpose=True,
                 )
 
-        for k in range(E // P):
+        for k in range(E_TILES):
             window = windows[k]
             es = slice(k * P, (k + 1) * P)
-            last = k == E // P - 1
+            last_rows = k == E_TILES - 1
             sum_banks = []
-            if not last:
-                for b in range(M // BANK):
+            if not last_rows:
+                for b in range(HALVES):
                     sum_banks.append(bank("pair_c"))
                     turn(sum_banks[b], faded[k], b, True, False)
             if k == 0:
-                deliver(k, 0, hi, "pair_a", windows[E // P])
-                for b in range(M // BANK):
-                    turn(sum_banks[b], windows[E // P], b, False, False)
-                deliver(k, hi, I, "pair_b", window)
+                deliver(k, 0, I // 2, "pair_a", windows[E_TILES])
+                for b in range(HALVES):
+                    turn(sum_banks[b], windows[E_TILES], b, False, False)
+                deliver(k, I // 2, I, "pair_b", window)
             else:
                 deliver(k, 0, I, ("pair_b", "pair_a")[k % 2], window)
             result = sb([P, M], F32, "result%d" % k)
-            if last:
-                for b in range(M // BANK):
+            if last_rows:
+                for b in range(HALVES):
                     bs = slice(b * BANK, (b + 1) * BANK)
                     nc.vector.tensor_tensor(out=result[:, bs], in0=faded[k][:, bs], in1=window[:, bs], op=ALU.add)
                     nc.sync.dma_start(out=out[es, bs], in_=result[:, bs])
             else:
                 turned_sum = ring.tile([P, M], F32, name="turned_sum")
-                for b in range(M // BANK):
+                for b in range(HALVES):
                     turn(sum_banks[b], window, b, False, True)
                     nc.scalar.copy(out=turned_sum[:, b * BANK : (b + 1) * BANK], in_=sum_banks[b][:])
-                for b in range(M // BANK):
+                for b in range(HALVES):
                     bs = slice(b * BANK, (b + 1) * BANK)
                     back = bank("pair_d")
-                    for jj in range(per_bank):
-                        j = b * per_bank + jj
-                        nc.tensor.transpose(back[:, jj * P : (jj + 1) * P], turned_sum[:, j * P : (j + 1) * P], ident[:])
+                    for jj in range(BLOCKS):
+                        j = b * BLOCKS + jj
+                        nc.tensor.transpose(
+                            back[:, jj * P : (jj + 1) * P], turned_sum[:, j * P : (j + 1) * P], ident[:]
+                        )
                     nc.scalar.copy(out=result[:, bs], in_=back[:])
                     nc.scalar.dma_start(out=out[es, bs], in_=result[:, bs])

from contextlib import ExitStack

import concourse.mybir as mybir
from concourse.masks import make_identity

D, T, I, Q, E, M = 512, 2048, 512, 512, 512, 1024
FLOPS = 2 * (3 * D * Q * I + Q * E * I)

F32 = mybir.dt.float32
BF16 = mybir.dt.bfloat16
I32 = mybir.dt.int32
U32 = mybir.dt.uint32
U16 = mybir.dt.uint16
U8 = mybir.dt.uint8
FP8X4 = mybir.dt.float8_e4m3fn_x4
FP4X4 = mybir.dt.float4_e2m1fn_x4
ALU = mybir.AluOpType
ACT = mybir.ActivationFunctionType
AX = mybir.AxisListType

P = 128
PACK = 4
RUNS = P // PACK
BANK = 512
BLOCKS = BANK // P
HALVES = M // BANK
E_TILES = E // P
LIST_ROWS = 16
QUADS, QUAD_ROWS, SCALE_ROWS = 4, 32, 4
ROW_EAGER, ROW_THRESH, ROW_QS = 0, 1, 2
VECTOR_TILES, SCALAR_TILES = (0, 1), (2, 3)
VECTOR_CLEARS = 3
EARLY_FADED = 2


def tile_attend_threeviews_abstaining_delivered_kernel(
    tc, query, query2, query3, keys_words, keys_scales, eager, thresh, qs, msgs, old, fade, offs, offs2, out
):
    nc = tc.nc
    with ExitStack() as ctx:
        keep = ctx.enter_context(tc.tile_pool(name="keep", bufs=1))
        ring = ctx.enter_context(tc.tile_pool(name="ring", bufs=2))
        psum = ctx.enter_context(tc.psum_pool(name="psum", bufs=2))

        def sb(shape, dtype, name):
            return keep.tile(shape, dtype, name=name, align_bytes=64)

        def bank(pair):
            return psum.tile([P, BANK], F32, name=pair)

        key_bytes = sb([P, T], U8, "key_bytes")
        nc.gpsimd.memset(key_bytes[:].bitcast(I32), 0)
        rows = sb([P, Q], F32, "rows")
        nc.vector.memset(rows[:], 0.0)
        windows = [sb([P, M], F32, "window%d" % w) for w in range(E_TILES + 1)]
        for w in windows[:VECTOR_CLEARS]:
            nc.vector.memset(w[:], 0.0)
        ident = sb([P, P], F32, "ident")
        make_identity(nc, ident[:])
        for w in windows[VECTOR_CLEARS:]:
            nc.gpsimd.memset(w[:], 0.0)

        key_list = keep.tile([P, I // LIST_ROWS], U16, name="key_list")
        nc.sync.dma_start(key_list[:], offs)
        key_words = sb([P, T], U16, "key_words")
        nc.sync.dma_start(out=key_words[:].bitcast(I32), in_=keys_words[0].bitcast(I32))
        for quad in range(QUADS):
            nc.sync.dma_start(
                out=key_bytes[QUAD_ROWS * quad : QUAD_ROWS * quad + SCALE_ROWS, :].bitcast(I32),
                in_=keys_scales[0, SCALE_ROWS * quad : SCALE_ROWS * (quad + 1), :].bitcast(I32),
            )
        fade_cols = sb([P, M // P], F32, "fade_cols")
        nc.sync.dma_start(out=fade_cols[:], in_=fade.rearrange("o (p j) -> (o p) j", p=P))
        raw3, raw2, raw1 = [sb([P, PACK, Q], F32, name) for name in ("raw3", "raw2", "raw1")]
        for src, dst in ((query3, raw3), (query2, raw2)):
            nc.sync.dma_start(out=dst[:], in_=src.rearrange("(p j) q -> p j q", j=PACK))
        for vec, row in ((eager, ROW_EAGER), (thresh, ROW_THRESH), (qs, ROW_QS)):
            nc.sync.dma_start(out=rows[row : row + 1, :], in_=vec.rearrange("q o -> o q"))
        nc.sync.dma_start(out=raw1[:], in_=query.rearrange("(p j) q -> p j q", j=PACK))
        raw_m = sb([P, PACK, E], F32, "raw_m")
        for r in range(PACK):
            nc.sync.dma_start(
                out=raw_m[:, r, :],
                in_=msgs.rearrange("(c r u) e -> r c u e", r=PACK, u=PACK)[r],
            )
        olds = []
        for k in range(E_TILES):
            old_tile = sb([P, M], F32, "old%d" % k)
            nc.sync.dma_start(out=old_tile[:], in_=old[k * P : (k + 1) * P, :])
            olds.append(old_tile)
        slot_list = keep.tile([P, I // LIST_ROWS], U16, name="slot_list")
        nc.sync.dma_start(slot_list[:], offs2)

        fade_rows = sb([P, P, M // P], F32, "fade_rows")
        for b in range(HALVES):
            fade_bank = bank("pair_c")
            for jj in range(BLOCKS):
                j = BLOCKS * b + jj
                nc.tensor.transpose(
                    fade_bank[:, jj * P : (jj + 1) * P], fade_cols[:, j : j + 1].to_broadcast([P, P]), ident[:]
                )
            nc.scalar.copy(
                out=fade_rows[:, :, BLOCKS * b : BLOCKS * (b + 1)], in_=fade_bank[:].rearrange("x (j p) -> x p j", p=P)
            )

        kw = sb([P, I], U16, "kw")
        nc.vector.tensor_copy(kw[:], key_words[:].indirect(key_list[:]))
        kb = sb([P, I], U8, "kb")
        nc.vector.tensor_copy(kb[:], key_bytes[:].indirect(key_list[:]))

        def woven(name):
            return sb([P, PACK, RUNS, PACK, PACK], BF16, name)

        def quantised(name, width):
            return sb([P, width], U32, name + "_codes"), sb([P, width], U8, name + "_scales")

        def quantise(dst, src, lo, hi):
            nc.vector.quantize_mx(
                out=dst[0][:, lo:hi].bitcast(FP8X4), scales=dst[1][:, lo:hi], in_=src[:, PACK * lo : PACK * hi]
            )

        w3, w2, w1 = woven("w3"), woven("w2"), woven("w1")
        q3, q2, q1 = quantised("q3", Q), quantised("q2", Q), quantised("q1", Q)
        flat = "p r c u j -> p (r c u j)"

        def dealt(raw):
            return raw[:].rearrange("p j (c r u) -> p r c j u", r=PACK, u=PACK)

        def weave_scalar(dst, raw, r, sign):
            nc.scalar.activation(
                out=dst[:, r].rearrange("p c u j -> p c j u"), in_=dealt(raw)[:, r], func=ACT.Copy, scale=sign
            )

        def weave_vector(dst, raw, r, sign):
            nc.vector.tensor_scalar(
                out=dst[:, r].rearrange("p c u j -> p c j u"), in0=dealt(raw)[:, r],
                scalar1=sign, scalar2=None, op0=ALU.mult,
            )

        def quantise_tiles(codes, src, tiles):
            quantise(codes, src[:].rearrange(flat), tiles[0] * P, (tiles[-1] + 1) * P)

        for dst, raw, codes, sign in ((w3, raw3, q3, -1.0), (w2, raw2, q2, 1.0)):
            for r in SCALAR_TILES:
                weave_scalar(dst, raw, r, sign)
            for r in VECTOR_TILES:
                weave_vector(dst, raw, r, sign)
            for tiles in (VECTOR_TILES, SCALAR_TILES):
                quantise_tiles(codes, dst, tiles)
        for r in VECTOR_TILES:
            weave_vector(w1, raw1, r, 1.0)
        quantise_tiles(q1, w1, VECTOR_TILES)

        dealt_rows = sb([P, PACK, RUNS, PACK], F32, "dealt_rows")
        nc.scalar.copy(out=dealt_rows[:], in_=rows[:].rearrange("v (c r u) -> v r c u", r=PACK, u=PACK))

        def score(dst, src, r, start, stop):
            cols = slice(r * P, (r + 1) * P)
            nc.tensor.matmul_mx(
                out=dst[:], lhsT=src[0][:, cols].bitcast(FP8X4), lhsT_scale=src[1][:, cols],
                rhs=kw[:].bitcast(FP4X4), rhs_scale=kb[:], start=start, stop=stop,
            )

        tanhs = []
        diffs = [bank(("pair_a", "pair_b")[r % 2]) for r in range(PACK)]
        for r in range(PACK):
            score(diffs[r], q3, r, True, False)
        for r in range(PACK):
            score(diffs[r], q2, r, False, True)
            th = sb([P, I], F32, "tanh%d" % r)
            nc.scalar.activation(out=th[:], in_=diffs[r][:], func=ACT.Tanh, scale=0.5)
            tanhs.append(th)
            if r < len(SCALAR_TILES):
                weave_scalar(w1, raw1, SCALAR_TILES[r], 1.0)
        quantise_tiles(q1, w1, SCALAR_TILES)

        a_banks, nb3_banks = [], []
        for r in range(PACK):
            a_banks.append(bank(("pair_c", "pair_d")[r % 2]))
            score(a_banks[r], q1, r, True, True)
            nb3_banks.append(bank(("pair_a", "pair_b")[r % 2]))
            score(nb3_banks[r], q3, r, True, True)

        turned = bank("pair_a")
        for r in range(PACK):
            nc.tensor.transpose(
                turned[:, r * P : (r + 1) * P], dealt_rows[:, r].rearrange("v c u -> v (c u)"), ident[:]
            )

        def columns(name, row, scale):
            cols_tile = sb([P, PACK], F32, name)
            nc.scalar.activation(out=cols_tile[:], in_=turned[:, row:BANK:P], func=ACT.Copy, scale=scale)
            return cols_tile

        mean_cols = columns("mean_cols", ROW_EAGER, -0.5 / I)
        thresh_cols = columns("thresh_cols", ROW_THRESH, -0.5)
        eager_cols = columns("eager_cols", ROW_EAGER, -0.5)
        half_qs = columns("half_qs", ROW_QS, 0.5)

        planes = sb([P, PACK, I], BF16, "planes")

        wm = sb([P, E, PACK], BF16, "wm")
        qm = quantised("qm", E)
        for k in range(E_TILES):
            cols = slice(k * P, (k + 1) * P)
            nc.gpsimd.tensor_scalar(
                out=wm[:, cols, :], in0=raw_m[:, :, cols].rearrange("p r e -> p e r"),
                scalar1=1.0, scalar2=0.0, op0=ALU.mult, op1=ALU.add,
            )

        def fading(dst, k):
            for b in range(HALVES):
                bs = slice(b * BANK, (b + 1) * BANK)
                nc.gpsimd.tensor_tensor(
                    out=dst[:, bs], in0=olds[k][:, bs],
                    in1=fade_rows[:].rearrange("x p j -> x (p j)")[:, bs], op=ALU.mult,
                )

        faded = [sb([P, M], F32, "faded%d" % k)[:] for k in range(EARLY_FADED)]
        for k in range(EARLY_FADED):
            fading(faded[k], k)

        for r in range(PACK):
            col = slice(r, r + 1)
            last_tile = r == PACK - 1
            twice = sb([P, I], F32, "twice%d" % r)
            nc.vector.scalar_tensor_tensor(
                out=twice[:], in0=tanhs[r][:], scalar=1.0, in1=a_banks[r][:], op0=ALU.add, op1=ALU.mult
            )
            s = sb([P, I], F32, "s%d" % r)
            s_sum = sb([P, 1], F32, "s_sum%d" % r)
            nc.vector.scalar_tensor_tensor(
                out=s[:], in0=twice[:], scalar=0.5, in1=nb3_banks[r][:], op0=ALU.mult, op1=ALU.subtract,
                accum_out=s_sum[:],
            )
            gate_bias = sb([P, 1], F32, "gate_bias%d" % r)
            nc.scalar.activation(
                out=gate_bias[:], in_=s_sum[:], func=ACT.Identity, scale=mean_cols[:, col], bias=thresh_cols[:, col]
            )
            neg_max = sb([P, 1], F32, "neg_max%d" % r)
            nc.vector.tensor_reduce(out=neg_max[:], in_=s[:], axis=AX.X, op=ALU.max, negate=True)
            gate = sb([P, 1], F32, "gate%d" % r)
            nc.scalar.activation(
                out=gate[:], in_=neg_max[:], func=ACT.Tanh, scale=eager_cols[:, col], bias=gate_bias[:]
            )
            expd = sb([P, I], F32, "p%d" % r)
            exp_sum = sb([P, 1], F32, "p_sum%d" % r)
            nc.scalar.activation(out=expd[:], in_=s[:], func=ACT.Exp, bias=neg_max[:], accum_out=exp_sum[:])
            gq = sb([P, 1], F32, "gq%d" % r)
            nc.scalar.activation(
                out=gq[:], in_=gate[:], func=ACT.Identity, scale=half_qs[:, col], bias=half_qs[:, col]
            )
            if last_tile:
                quantise(qm, wm[:].rearrange("p e r -> p (e r)"), 0, E)
            inv = sb([P, 1], F32, "inv%d" % r)
            nc.vector.reciprocal(out=inv[:], in_=exp_sum[:])
            if last_tile:
                nc.vector.tensor_scalar(
                    out=planes[:, r, :], in0=expd[:], scalar1=inv[:], scalar2=gq[:], op0=ALU.mult, op1=ALU.mult
                )
            else:
                factor = sb([P, 1], F32, "factor%d" % r)
                nc.scalar.activation(out=factor[:], in_=inv[:], func=ACT.Copy, scale=gq[:])
                nc.scalar.activation(out=planes[:, r, :], in_=expd[:], func=ACT.Copy, scale=factor[:])

        ww = sb([P, I, PACK], BF16, "ww")
        qw = quantised("qw", I)
        for h in range(I // P):
            cols = slice(h * P, (h + 1) * P)
            nc.vector.tensor_copy(
                out=ww[:, cols, :].rearrange("p (c i) r -> p c r i", i=PACK),
                in_=planes[:, :, cols].rearrange("p r (c i) -> p c r i", i=PACK),
            )
            quantise(qw, ww[:].rearrange("p i r -> p (i r)"), h * P, (h + 1) * P)

        late = keep.tile([P, E_TILES - EARLY_FADED, M], F32, name="faded_late", tag="ww", align_bytes=64)
        for k in range(EARLY_FADED, E_TILES):
            faded.append(late[:, k - EARLY_FADED, :])
            fading(faded[k], k)

        def deliver(k, lo, hi, pair, window):
            cols = slice(k * P, (k + 1) * P)
            dl_bank = bank(pair)
            nc.tensor.matmul_mx(
                out=dl_bank[:, 0 : hi - lo], lhsT=qm[0][:, cols].bitcast(FP8X4), lhsT_scale=qm[1][:, cols],
                rhs=qw[0][:, lo:hi].bitcast(FP8X4), rhs_scale=qw[1][:, lo:hi], start=True, stop=True,
            )
            dl = sb([P, hi - lo], F32, "dl%d_%d" % (k, lo))
            nc.scalar.copy(out=dl[:], in_=dl_bank[:, 0 : hi - lo])
            nc.vector.tensor_copy(window[:].indirect(slot_list[:, lo // LIST_ROWS : hi // LIST_ROWS]), dl[:])

        def turn(dst, src, b, start, stop):
            for jj in range(BLOCKS):
                j = b * BLOCKS + jj
                nc.tensor.matmul(
                    dst[:, jj * P : (jj + 1) * P], src[:, j * P : (j + 1) * P], ident[:],
                    start=start and jj == 0, stop=stop and jj == BLOCKS - 1, is_transpose=True,
                )

        for k in range(E_TILES):
            window = windows[k]
            es = slice(k * P, (k + 1) * P)
            last_rows = k == E_TILES - 1
            sum_banks = []
            if not last_rows:
                for b in range(HALVES):
                    sum_banks.append(bank("pair_c"))
                    turn(sum_banks[b], faded[k], b, True, False)
            if k == 0:
                deliver(k, 0, I // 2, "pair_a", windows[E_TILES])
                for b in range(HALVES):
                    turn(sum_banks[b], windows[E_TILES], b, False, False)
                deliver(k, I // 2, I, "pair_b", window)
            else:
                deliver(k, 0, I, ("pair_b", "pair_a")[k % 2], window)
            result = sb([P, M], F32, "result%d" % k)
            if last_rows:
                for b in range(HALVES):
                    bs = slice(b * BANK, (b + 1) * BANK)
                    nc.vector.tensor_tensor(out=result[:, bs], in0=faded[k][:, bs], in1=window[:, bs], op=ALU.add)
                    nc.sync.dma_start(out=out[es, bs], in_=result[:, bs])
            else:
                turned_sum = ring.tile([P, M], F32, name="turned_sum")
                for b in range(HALVES):
                    turn(sum_banks[b], window, b, False, True)
                    nc.scalar.copy(out=turned_sum[:, b * BANK : (b + 1) * BANK], in_=sum_banks[b][:])
                for b in range(HALVES):
                    bs = slice(b * BANK, (b + 1) * BANK)
                    back = bank("pair_d")
                    for jj in range(BLOCKS):
                        j = b * BLOCKS + jj
                        nc.tensor.transpose(
                            back[:, jj * P : (jj + 1) * P], turned_sum[:, j * P : (j + 1) * P], ident[:]
                        )
                    nc.scalar.copy(out=result[:, bs], in_=back[:])
                    nc.scalar.dma_start(out=out[es, bs], in_=result[:, bs])
